import numpy as np, ml_dtypes
CORES = [1,3,5,7,9,11,13,15,17,19,21,23,25,27,29,31,33,35,37,39,41,43,45,47,49,51,53,55,57,59,61,63]
N = 32
def setup_inputs(rng):
    return {"x": rng.standard_normal((N, 128, 16), dtype=np.float32).astype(ml_dtypes.bfloat16)}
def reference(x):
    s = x.min(axis=0)
    return {"y": np.broadcast_to(s, (N,) + s.shape)}

@@ -1,0 +1,52 @@
+import concourse.bass as bass
+
+W = 16
+FOLDER = 2
+
+SCRATCH = {
+    "mine": ("sbuf", [128, W], "bfloat16"),
+    "gath": ("sbuf", [128, 4 * W], "bfloat16"),
+    "part": ("sbuf", [128, 8 * W], "bfloat16"),
+    "res": ("sbuf", [128, W], "bfloat16"),
+}
+SEMAPHORES = ["ld", "st", "a1", "a2", "a3", "sent"]
+
+
+def slot(buf, j):
+    return buf[:, j * W:(j + 1) * W]
+
+
+def rank_program(g, core, T, topo):
+    chip, k = divmod(core, 8)
+
+    def dst(c):
+        rid, pid, se = topo.addr(c)
+        return bass.DstId(rid=rid, pnc=pid)
+
+    if T.rank_of(core) is not None:
+        g.dma_start(T.mine[:], T.x[:]).then_inc(T.sem.ld, 16)
+        g.wait_ge(T.sem.ld, 16)
+        rid, pid, se = topo.addr(chip * 8 + FOLDER)
+        g.remote_dma(slot(T.gath, k // 2), T.mine[:], T.sem.a1, T.sem.sent, pid, rid, 0xFFFF)
+        g.wait_ge(T.sem.a3, 16)
+        g.dma_start(T.y[:], T.res[:]).then_inc(T.sem.st, 16)
+        g.wait_ge(T.sem.st, 16)
+        g.wait_ge(T.sem.sent, 16)
+        return
+
+    if k != FOLDER:
+        return
+
+    own = [slot(T.gath, j) for j in range(4)]
+    others = [c for c in range(8) if c != chip]
+    g.wait_ge(T.sem.a1, 4 * 16)
+    g.remote_dma_fused([bass.RemoteDMATransfer(
+        dst_ids=[dst(c * 8 + FOLDER) for c in others], dma_engine_mask=0x00FF, remote_sem=T.sem.a2,
+        srcs=own, dsts=[slot(T.part, chip) for c in others], alu_op=3)], local_sem=T.sem.sent)
+    g.wait_ge(T.sem.a2, 7 * 8)
+    ranks = [chip * 8 + j for j in (1, 3, 5, 7)]
+    g.remote_dma_fused([bass.RemoteDMATransfer(
+        dst_ids=[dst(c) for c in ranks], dma_engine_mask=0xFFFF, remote_sem=T.sem.a3,
+        srcs=own + [slot(T.part, c) for c in others], dsts=[T.res[:] for c in ranks], alu_op=3)],
+        local_sem=T.sem.sent)
+    g.wait_ge(T.sem.sent, 8 + 16)

@@ -4,16 +4,16 @@ W = 16
 FOLDER = 2
 
 SCRATCH = {
-    "mine": ("sbuf", [128, W], "bfloat16"),
-    "gath": ("sbuf", [128, 4 * W], "bfloat16"),
-    "part": ("sbuf", [128, 8 * W], "bfloat16"),
-    "res": ("sbuf", [128, W], "bfloat16"),
+    "mine": ("dram", [128, W], "bfloat16"),
+    "gath": ("dram", [4, 128, W], "bfloat16"),
+    "part": ("dram", [8, 128, W], "bfloat16"),
+    "res": ("dram", [128, W], "bfloat16"),
 }
 SEMAPHORES = ["ld", "st", "a1", "a2", "a3", "sent"]
 
 
 def slot(buf, j):
-    return buf[:, j * W:(j + 1) * W]
+    return buf[j]
 
 
 def rank_program(g, core, T, topo):

@@ -1,23 +1,21 @@
 import concourse.bass as bass
 
 W = 16
-FOLDER = 2
+FOLDERS = (2, 6)
+FINISHER = 0
 
 SCRATCH = {
     "mine": ("dram", [128, W], "bfloat16"),
-    "gath": ("dram", [4, 128, W], "bfloat16"),
-    "part": ("dram", [8, 128, W], "bfloat16"),
+    "gath": ("dram", [8, 128, W], "bfloat16"),
+    "part": ("dram", [4, 128, W], "bfloat16"),
     "res": ("dram", [128, W], "bfloat16"),
 }
 SEMAPHORES = ["ld", "st", "a1", "a2", "a3", "sent"]
 
 
-def slot(buf, j):
-    return buf[j]
-
-
 def rank_program(g, core, T, topo):
     chip, k = divmod(core, 8)
+    par, half = chip & 1, k // 4
 
     def dst(c):
         rid, pid, se = topo.addr(c)
@@ -26,27 +24,37 @@ def rank_program(g, core, T, topo):
     if T.rank_of(core) is not None:
         g.dma_start(T.mine[:], T.x[:]).then_inc(T.sem.ld, 16)
         g.wait_ge(T.sem.ld, 16)
-        rid, pid, se = topo.addr(chip * 8 + FOLDER)
-        g.remote_dma(slot(T.gath, k // 2), T.mine[:], T.sem.a1, T.sem.sent, pid, rid, 0xFFFF)
+        j = (chip // 2) * 2 + (k % 4) // 2
+        away = [c for c in range(par, 8, 2) if c != chip]
+        g.remote_dma_fused([
+            bass.RemoteDMATransfer(
+                dst_ids=[dst(c * 8 + FOLDERS[half]) for c in away], dma_engine_mask=0x00FF, remote_sem=T.sem.a1,
+                srcs=[T.mine[:]], dsts=[T.gath[j] for c in away], alu_op=0),
+            bass.RemoteDMATransfer(
+                dst_ids=[dst(chip * 8 + FOLDERS[half])], dma_engine_mask=0xFF00, remote_sem=T.sem.a1,
+                srcs=[T.mine[:]], dsts=[T.gath[j]], alu_op=0),
+        ], local_sem=T.sem.sent)
         g.wait_ge(T.sem.a3, 16)
         g.dma_start(T.y[:], T.res[:]).then_inc(T.sem.st, 16)
         g.wait_ge(T.sem.st, 16)
         g.wait_ge(T.sem.sent, 16)
         return
 
-    if k != FOLDER:
+    if k in FOLDERS:
+        to = [chip * 8 + FINISHER, (chip ^ 1) * 8 + FINISHER]
+        g.wait_ge(T.sem.a1, 8 * 8)
+        g.remote_dma_fused([bass.RemoteDMATransfer(
+            dst_ids=[dst(c) for c in to], dma_engine_mask=0x00FF, remote_sem=T.sem.a2,
+            srcs=[T.gath[j] for j in range(8)], dsts=[T.part[2 * par + half] for c in to], alu_op=3)],
+            local_sem=T.sem.sent)
+        g.wait_ge(T.sem.sent, 8)
         return
 
-    own = [slot(T.gath, j) for j in range(4)]
-    others = [c for c in range(8) if c != chip]
-    g.wait_ge(T.sem.a1, 4 * 16)
-    g.remote_dma_fused([bass.RemoteDMATransfer(
-        dst_ids=[dst(c * 8 + FOLDER) for c in others], dma_engine_mask=0x00FF, remote_sem=T.sem.a2,
-        srcs=own, dsts=[slot(T.part, chip) for c in others], alu_op=3)], local_sem=T.sem.sent)
-    g.wait_ge(T.sem.a2, 7 * 8)
-    ranks = [chip * 8 + j for j in (1, 3, 5, 7)]
-    g.remote_dma_fused([bass.RemoteDMATransfer(
-        dst_ids=[dst(c) for c in ranks], dma_engine_mask=0xFFFF, remote_sem=T.sem.a3,
-        srcs=own + [slot(T.part, c) for c in others], dsts=[T.res[:] for c in ranks], alu_op=3)],
-        local_sem=T.sem.sent)
-    g.wait_ge(T.sem.sent, 8 + 16)
+    if k == FINISHER:
+        ranks = [chip * 8 + j for j in (1, 3, 5, 7)]
+        g.wait_ge(T.sem.a2, 4 * 8)
+        g.remote_dma_fused([bass.RemoteDMATransfer(
+            dst_ids=[dst(c) for c in ranks], dma_engine_mask=0xFFFF, remote_sem=T.sem.a3,
+            srcs=[T.part[j] for j in range(4)], dsts=[T.res[:] for c in ranks], alu_op=3)],
+            local_sem=T.sem.sent)
+        g.wait_ge(T.sem.sent, 16)

@@ -41,7 +41,7 @@ def rank_program(g, core, T, topo):
         return
 
     if k in FOLDERS:
-        to = [chip * 8 + FINISHER, (chip ^ 1) * 8 + FINISHER]
+        to = [(chip ^ 1) * 8 + FINISHER, chip * 8 + FINISHER]
         g.wait_ge(T.sem.a1, 8 * 8)
         g.remote_dma_fused([bass.RemoteDMATransfer(
             dst_ids=[dst(c) for c in to], dma_engine_mask=0x00FF, remote_sem=T.sem.a2,

@@ -25,19 +25,14 @@ def rank_program(g, core, T, topo):
         g.dma_start(T.mine[:], T.x[:]).then_inc(T.sem.ld, 16)
         g.wait_ge(T.sem.ld, 16)
         j = (chip // 2) * 2 + (k % 4) // 2
-        away = [c for c in range(par, 8, 2) if c != chip]
-        g.remote_dma_fused([
-            bass.RemoteDMATransfer(
-                dst_ids=[dst(c * 8 + FOLDERS[half]) for c in away], dma_engine_mask=0x00FF, remote_sem=T.sem.a1,
-                srcs=[T.mine[:]], dsts=[T.gath[j] for c in away], alu_op=0),
-            bass.RemoteDMATransfer(
-                dst_ids=[dst(chip * 8 + FOLDERS[half])], dma_engine_mask=0xFF00, remote_sem=T.sem.a1,
-                srcs=[T.mine[:]], dsts=[T.gath[j]], alu_op=0),
-        ], local_sem=T.sem.sent)
+        chips = [c for c in range(par, 8, 2) if c != chip] + [chip]
+        g.remote_dma_fused([bass.RemoteDMATransfer(
+            dst_ids=[dst(c * 8 + FOLDERS[half]) for c in chips], dma_engine_mask=0x00FF, remote_sem=T.sem.a1,
+            srcs=[T.mine[:]], dsts=[T.gath[j] for c in chips], alu_op=0)], local_sem=T.sem.sent)
         g.wait_ge(T.sem.a3, 16)
         g.dma_start(T.y[:], T.res[:]).then_inc(T.sem.st, 16)
         g.wait_ge(T.sem.st, 16)
-        g.wait_ge(T.sem.sent, 16)
+        g.wait_ge(T.sem.sent, 8)
         return
 
     if k in FOLDERS:

@@ -1,13 +1,14 @@
 import concourse.bass as bass
 
 W = 16
-FOLDERS = (2, 6)
-FINISHER = 0
+SW_FIRST = (2, 6)
+MATE_FIRST = 0
+FINISHER = 4
 
 SCRATCH = {
     "mine": ("dram", [128, W], "bfloat16"),
-    "gath": ("dram", [8, 128, W], "bfloat16"),
-    "part": ("dram", [4, 128, W], "bfloat16"),
+    "gath": ("dram", [4, 128, W], "bfloat16"),
+    "part": ("dram", [8, 128, W], "bfloat16"),
     "res": ("dram", [128, W], "bfloat16"),
 }
 SEMAPHORES = ["ld", "st", "a1", "a2", "a3", "sent"]
@@ -15,41 +16,36 @@ SEMAPHORES = ["ld", "st", "a1", "a2", "a3", "sent"]
 
 def rank_program(g, core, T, topo):
     chip, k = divmod(core, 8)
-    par, half = chip & 1, k // 4
+    par, pair, half = chip & 1, chip // 2, k // 4
+    plane = [(chip + 2 * i) % 8 for i in (1, 2, 3, 0)]
+    mates = [chip ^ 1, chip]
 
-    def dst(c):
-        rid, pid, se = topo.addr(c)
-        return bass.DstId(rid=rid, pnc=pid)
+    def send(srcs, cores, where, sem, mask):
+        ids = [topo.addr(c) for c in cores]
+        g.remote_dma_fused([bass.RemoteDMATransfer(
+            dst_ids=[bass.DstId(rid=a[0], pnc=a[1]) for a in ids], dma_engine_mask=mask, remote_sem=sem,
+            srcs=srcs, dsts=[where for c in cores], alu_op=3 if len(srcs) > 1 else 0)], local_sem=T.sem.sent)
 
     if T.rank_of(core) is not None:
         g.dma_start(T.mine[:], T.x[:]).then_inc(T.sem.ld, 16)
         g.wait_ge(T.sem.ld, 16)
-        j = (chip // 2) * 2 + (k % 4) // 2
-        chips = [c for c in range(par, 8, 2) if c != chip] + [chip]
-        g.remote_dma_fused([bass.RemoteDMATransfer(
-            dst_ids=[dst(c * 8 + FOLDERS[half]) for c in chips], dma_engine_mask=0x00FF, remote_sem=T.sem.a1,
-            srcs=[T.mine[:]], dsts=[T.gath[j] for c in chips], alu_op=0)], local_sem=T.sem.sent)
+        if k % 4 == 1:
+            send([T.mine[:]], [c * 8 + SW_FIRST[half] for c in plane], T.gath[pair], T.sem.a1, 0x00FF)
+        else:
+            send([T.mine[:]], [c * 8 + MATE_FIRST for c in mates], T.gath[2 * par + half], T.sem.a1, 0x00FF)
         g.wait_ge(T.sem.a3, 16)
         g.dma_start(T.y[:], T.res[:]).then_inc(T.sem.st, 16)
         g.wait_ge(T.sem.st, 16)
         g.wait_ge(T.sem.sent, 8)
-        return
-
-    if k in FOLDERS:
-        to = [(chip ^ 1) * 8 + FINISHER, chip * 8 + FINISHER]
-        g.wait_ge(T.sem.a1, 8 * 8)
-        g.remote_dma_fused([bass.RemoteDMATransfer(
-            dst_ids=[dst(c) for c in to], dma_engine_mask=0x00FF, remote_sem=T.sem.a2,
-            srcs=[T.gath[j] for j in range(8)], dsts=[T.part[2 * par + half] for c in to], alu_op=3)],
-            local_sem=T.sem.sent)
+    elif k in SW_FIRST:
+        g.wait_ge(T.sem.a1, 4 * 8)
+        send([T.gath[j] for j in range(4)], [c * 8 + FINISHER for c in mates], T.part[2 * par + half], T.sem.a2, 0x00FF)
         g.wait_ge(T.sem.sent, 8)
-        return
-
-    if k == FINISHER:
-        ranks = [chip * 8 + j for j in (1, 3, 5, 7)]
-        g.wait_ge(T.sem.a2, 4 * 8)
-        g.remote_dma_fused([bass.RemoteDMATransfer(
-            dst_ids=[dst(c) for c in ranks], dma_engine_mask=0xFFFF, remote_sem=T.sem.a3,
-            srcs=[T.part[j] for j in range(4)], dsts=[T.res[:] for c in ranks], alu_op=3)],
-            local_sem=T.sem.sent)
+    elif k == MATE_FIRST:
+        g.wait_ge(T.sem.a1, 4 * 8)
+        send([T.gath[j] for j in range(4)], [c * 8 + FINISHER for c in plane], T.part[4 + pair], T.sem.a2, 0x00FF)
+        g.wait_ge(T.sem.sent, 8)
+    elif k == FINISHER:
+        g.wait_ge(T.sem.a2, 8 * 8)
+        send([T.part[j] for j in range(8)], [chip * 8 + j for j in (1, 3, 5, 7)], T.res[:], T.sem.a3, 0xFFFF)
         g.wait_ge(T.sem.sent, 16)

import concourse.bass as bass

W = 16
SW_FIRST = (2, 6)
MATE_FIRST = 0
FINISHER = 4

SCRATCH = {
    "mine": ("dram", [128, W], "bfloat16"),
    "gath": ("dram", [4, 128, W], "bfloat16"),
    "part": ("dram", [8, 128, W], "bfloat16"),
    "res": ("dram", [128, W], "bfloat16"),
}
SEMAPHORES = ["ld", "st", "a1", "a2", "a3", "sent"]


def rank_program(g, core, T, topo):
    chip, k = divmod(core, 8)
    par, pair, half = chip & 1, chip // 2, k // 4
    plane = [(chip + 2 * i) % 8 for i in (1, 2, 3, 0)]
    mates = [chip ^ 1, chip]

    def send(srcs, cores, where, sem, mask):
        ids = [topo.addr(c) for c in cores]
        g.remote_dma_fused([bass.RemoteDMATransfer(
            dst_ids=[bass.DstId(rid=a[0], pnc=a[1]) for a in ids], dma_engine_mask=mask, remote_sem=sem,
            srcs=srcs, dsts=[where for c in cores], alu_op=3 if len(srcs) > 1 else 0)], local_sem=T.sem.sent)

    if T.rank_of(core) is not None:
        g.dma_start(T.mine[:], T.x[:]).then_inc(T.sem.ld, 16)
        g.wait_ge(T.sem.ld, 16)
        if k % 4 == 1:
            send([T.mine[:]], [c * 8 + SW_FIRST[half] for c in plane], T.gath[pair], T.sem.a1, 0x00FF)
        else:
            send([T.mine[:]], [c * 8 + MATE_FIRST for c in mates], T.gath[2 * par + half], T.sem.a1, 0x00FF)
        g.wait_ge(T.sem.a3, 16)
        g.dma_start(T.y[:], T.res[:]).then_inc(T.sem.st, 16)
        g.wait_ge(T.sem.st, 16)
        g.wait_ge(T.sem.sent, 8)
    elif k in SW_FIRST:
        g.wait_ge(T.sem.a1, 4 * 8)
        send([T.gath[j] for j in range(4)], [c * 8 + FINISHER for c in mates], T.part[2 * par + half], T.sem.a2, 0x00FF)
        g.wait_ge(T.sem.sent, 8)
    elif k == MATE_FIRST:
        g.wait_ge(T.sem.a1, 4 * 8)
        send([T.gath[j] for j in range(4)], [c * 8 + FINISHER for c in plane], T.part[4 + pair], T.sem.a2, 0x00FF)
        g.wait_ge(T.sem.sent, 8)
    elif k == FINISHER:
        g.wait_ge(T.sem.a2, 8 * 8)
        send([T.part[j] for j in range(8)], [chip * 8 + j for j in (1, 3, 5, 7)], T.res[:], T.sem.a3, 0xFFFF)
        g.wait_ge(T.sem.sent, 16)
